import numpy as np
import ml_dtypes


def mxq(x, axis, fmt="e4m3"):
    dtype, down = {"e4m3": (ml_dtypes.float8_e4m3fn, 7), "e5m2": (ml_dtypes.float8_e5m2, 14)}[fmt]
    v = np.moveaxis(np.asarray(x, np.float32).astype(ml_dtypes.bfloat16).astype(np.float64), axis, -1)
    blocks = v.reshape(v.shape[:-1] + (-1, 32))
    amax = np.abs(blocks).max(-1, keepdims=True)
    byte = np.maximum(np.where(amax > 0, np.frexp(amax)[1] - 1 + 127, 0) - down, 1)
    scale = np.exp2(byte - 127.0)
    codes = (blocks / scale).astype(np.float32).astype(dtype).astype(np.float64)
    return np.moveaxis((codes * scale).reshape(v.shape), -1, axis)


WIDE = False


def mx_kscale(k):
    if not WIDE:
        return np.ones(k)
    levels = np.array([30, -30])
    if k % 512:
        return np.exp2(np.random.permutation(np.resize(levels, k // 32))).repeat(32)
    a = np.empty((k // 512, 16))
    for p in range(k // 512):
        a[p, :8] = np.random.permutation(np.resize(levels, 8))
        for g in range(8):
            far = levels[np.abs(levels - a[p, g]) >= 10]
            a[p, g + 8] = far[np.random.randint(len(far))]
    return np.exp2(a.ravel()).repeat(32)


def f64(x):
    return np.asarray(x).astype(np.float64)


E2M1 = np.array([0.0, 0.5, 1.0, 1.5, 2.0, 3.0, 4.0, 6.0, -0.0, -0.5, -1.0, -1.5, -2.0, -3.0, -4.0, -6.0])


def pack_weight(w, fmt):
    k, n = w.shape
    w = f64(np.asarray(w, np.float32).astype(ml_dtypes.bfloat16)).reshape(k // 32, 32, n)
    amax = np.abs(w).max(1)
    if fmt == "e4m3":
        byte = np.frexp(amax)[1] - 1 + 127 - 7
    else:
        mant, ex = np.frexp(amax / 6.0)
        byte = np.where(mant > 0.5, ex, ex - 1) + 127
    byte = np.clip(np.where(amax > 0, byte, 1), 1, 254)
    scaled = (w * np.exp2(127.0 - byte)[:, None, :]).reshape(k, n).astype(np.float32)
    by_word = np.ascontiguousarray(scaled.reshape(k // 512, 128, 4, n).transpose(0, 1, 3, 2))
    if fmt == "e4m3":
        words = by_word.astype(ml_dtypes.float8_e4m3fn).view(np.uint8)
    else:
        c = by_word.astype(ml_dtypes.float4_e2m1fn).view(np.uint8) & 0xF
        words = (c[..., 0::2] | (c[..., 1::2] << 4)).reshape(k // 512, 128, 2 * n)
    return np.ascontiguousarray(words), np.ascontiguousarray(byte.astype(np.uint8).reshape(k // 512, 16, n))


def unpack_weight(words, scales, fmt):
    g, _, n = scales.shape
    words = np.ascontiguousarray(words).reshape(g, 128, n, -1)
    if fmt == "e4m3":
        vals = words.view(ml_dtypes.float8_e4m3fn).astype(np.float64)
    else:
        nib = np.empty((g, 128, n, 4), np.uint8)
        nib[..., 0::2] = words & 0xF
        nib[..., 1::2] = words >> 4
        vals = E2M1[nib]
    vals = vals * np.repeat(np.exp2(scales.astype(np.float64) - 127.0), 8, axis=1)[..., None]
    return vals.transpose(0, 1, 3, 2).reshape(g * 512, n)


K, L, M, T, N = 512, 512, 512, 512, 512


def setup_inputs():
    n = np.random.standard_normal
    fk = mx_kscale(K)
    fl = mx_kscale(L)
    fm = mx_kscale(M)
    xtp = pack_weight(n((K, T)) / fk[:, None], "e4m3")
    wap = pack_weight(n((K, M)) * 1 / np.sqrt(K) * fk[:, None], "e2m1")
    xqp = pack_weight(n((L, T)) / fl[:, None], "e4m3")
    wcp = pack_weight(n((L, M)) * 1 / np.sqrt(L) * fl[:, None], "e2m1")
    wbp = pack_weight(n((K, M)) * 1 / np.sqrt(K) * fk[:, None], "e2m1")
    wep = pack_weight(n((L, M)) * 1 / np.sqrt(L) * fl[:, None], "e4m3")
    wtp = pack_weight(n((M, N)) * 1 / np.sqrt(M) / fm[:, None], "e4m3")
    return {
        "xt_words": xtp[0],
        "xt_scales": xtp[1],
        "wa_words": wap[0],
        "wa_scales": wap[1],
        "xq_words": xqp[0],
        "xq_scales": xqp[1],
        "wc_words": wcp[0],
        "wc_scales": wcp[1],
        "wb_words": wbp[0],
        "wb_scales": wbp[1],
        "we_words": wep[0],
        "we_scales": wep[1],
        "us": (np.random.uniform(0.5, 2.0, (M, 1)) * fm[:, None]).astype(np.float32),
        "wt_words": wtp[0],
        "wt_scales": wtp[1],
        "rw": (np.random.uniform(0.5, 2.0, (1, T))).astype(np.float32),
    }


def reference(xt_words, xt_scales, wa_words, wa_scales, xq_words, xq_scales, wc_words, wc_scales, wb_words, wb_scales, we_words, we_scales, us, wt_words, wt_scales, rw):
    xtu = unpack_weight(xt_words, xt_scales, "e4m3")
    wau = unpack_weight(wa_words, wa_scales, "e2m1")
    xqu = unpack_weight(xq_words, xq_scales, "e4m3")
    wcu = unpack_weight(wc_words, wc_scales, "e2m1")
    wbu = unpack_weight(wb_words, wb_scales, "e2m1")
    weu = unpack_weight(we_words, we_scales, "e4m3")
    wtu = unpack_weight(wt_words, wt_scales, "e4m3")
    p = wau.T @ xtu + wcu.T @ xqu
    q = wbu.T @ xtu + weu.T @ xqu
    d = np.tanh(p - q) * f64(us)
    dq = mxq(d, 0, "e5m2")
    b = wtu.T @ dq
    y = b * f64(rw)
    return y

@@ -1,0 +1,171 @@
+from contextlib import ExitStack
+
+import concourse.mybir as mybir
+from concourse.masks import make_identity
+
+F32 = mybir.dt.float32
+BF16 = mybir.dt.bfloat16
+I32 = mybir.dt.int32
+U32 = mybir.dt.uint32
+U8 = mybir.dt.uint8
+E4M3 = mybir.dt.float8_e4m3fn_x4
+E5M2 = mybir.dt.float8_e5m2_x4
+E2M1 = mybir.dt.float4_e2m1fn_x4
+ACT = mybir.ActivationFunctionType
+ALU = mybir.AluOpType
+
+P = 128
+D = 512
+PACK = 4
+TILES = D // P
+HALF = D // 2
+FLOPS = 5 * 2 * D * D * D
+
+
+def tile_mix_gap_of_two_sums_back_kernel(
+    tc, xt_words, xt_scales, wa_words, wa_scales, xq_words, xq_scales, wc_words, wc_scales,
+    wb_words, wb_scales, we_words, we_scales, us, wt_words, wt_scales, rw, out,
+):
+    nc = tc.nc
+    with ExitStack() as ctx:
+        sb = ctx.enter_context(tc.tile_pool(name="sb", bufs=1))
+        ps = ctx.enter_context(tc.psum_pool(name="ps", bufs=1))
+        ctx.enter_context(tc.manual_schedule())
+
+        def zeroed_planes(name, count):
+            planes = sb.tile([P, count, D], U8, name=name, align_bytes=64)
+            nc.vector.memset(planes[:].bitcast(I32), 0)
+            return planes
+
+        def stage_scales(name, scale_inputs):
+            staged = sb.tile([P, len(scale_inputs), D // 4], I32, name=name)
+            for i, scales in enumerate(scale_inputs):
+                nc.sync.dma_start(out=staged[16:32, i, :], in_=scales[0].bitcast(I32))
+            return staged
+
+        def spread_scales(planes, staged):
+            for q in range(4):
+                nc.sync.dma_start(
+                    out=planes[32 * q : 32 * q + 4].bitcast(I32), in_=staged[16 + 4 * q : 20 + 4 * q]
+                )
+
+        def load_codes(name, rows):
+            codes = sb.tile([P, rows.shape[1]], U8, name=name, align_bytes=64)
+            nc.sync.dma_start(out=codes[:].bitcast(I32), in_=rows.bitcast(I32))
+            return codes
+
+        def fp8_rows(words):
+            return words[0].rearrange("p n r -> p (n r)")
+
+        q_planes = zeroed_planes("q_planes", 4)
+        p_planes = zeroed_planes("p_planes", 2)
+        wt_plane = zeroed_planes("wt_plane", 1)
+        d_codes = sb.tile([P, HALF + D], U32, align_bytes=64)
+        d_scales = sb.tile([P, HALF + D], U8, align_bytes=64)
+        nc.vector.memset(d_codes[:, :HALF], 0)
+        nc.vector.memset(d_scales[:, :HALF].bitcast(U32), 0)
+        first = sb.tile([P, 2], F32)
+        nc.vector.memset(first[:, 0:1], 0.0)
+        nc.scalar.activation(out=first[:, 1:2], in_=first[:, 0:1], func=ACT.Tanh)
+        ident = sb.tile([P, P], F32)
+        make_identity(nc, ident[:])
+
+        q_staged = stage_scales("q_staged", (xt_scales, wb_scales, xq_scales, we_scales))
+        xt = load_codes("xt", fp8_rows(xt_words))
+        wb = load_codes("wb", wb_words[0])
+        xq = load_codes("xq", fp8_rows(xq_words))
+        we = load_codes("we", fp8_rows(we_words))
+        spread_scales(q_planes, q_staged)
+        p_staged = stage_scales("p_staged", (wa_scales, wc_scales))
+        wa = load_codes("wa", wa_words[0])
+        wc = load_codes("wc", wc_words[0])
+        spread_scales(p_planes, p_staged)
+        wt_staged = stage_scales("wt_staged", (wt_scales,))
+        us_sb = sb.tile([P, PACK], F32)
+        nc.sync.dma_start(out=us_sb[:], in_=us.rearrange("(p j) o -> p (j o)", j=PACK))
+        wt = load_codes("wt", fp8_rows(wt_words))
+        spread_scales(wt_plane, wt_staged)
+        rw_sb = sb.tile([P, D], F32)
+        nc.sync.dma_start(out=rw_sb[:], in_=rw[0].partition_broadcast(P))
+        xt_s, wb_s, xq_s, we_s = [q_planes[:, i, :] for i in range(4)]
+        wa_s, wc_s = [p_planes[:, i, :] for i in range(2)]
+        wt_s = wt_plane[:, 0, :]
+
+        def bank(i):
+            acc = ps.tile([P, D], F32, name="acc", tag="bank%d" % i)
+            return acc
+
+        def product(acc, c, x, x_s, w, w_s, w_dtype, opens):
+            nc.tensor.matmul_mx(
+                out=acc[:],
+                lhsT=x[:, c * PACK * P : (c + 1) * PACK * P].bitcast(E4M3),
+                lhsT_scale=x_s[:, c * P : (c + 1) * P],
+                rhs=w[:].bitcast(w_dtype),
+                rhs_scale=w_s,
+                start=opens,
+                stop=not opens,
+            )
+
+        def by_slot(acc):
+            return acc[:].rearrange("t (p j) -> t j p", j=PACK)
+
+        q_acc = [bank(c) for c in range(TILES)]
+        for c in range(TILES):
+            product(q_acc[c], c, xt, xt_s, wb, wb_s, E2M1, True)
+        q_sb = []
+        for c in range(TILES):
+            product(q_acc[c], c, xq, xq_s, we, we_s, E4M3, False)
+            q_sb.append(sb.tile([P, PACK, P], F32, name="q_sb%d" % c))
+            nc.scalar.copy(out=q_sb[c][:], in_=by_slot(q_acc[c]))
+
+        th = []
+        for c in range(TILES):
+            p_acc = bank(TILES + c)
+            product(p_acc, c, xt, xt_s, wa, wa_s, E2M1, True)
+            product(p_acc, c, xq, xq_s, wc, wc_s, E2M1, False)
+            gap = sb.tile([P, PACK, P], F32, name="gap%d" % c)
+            nc.vector.tensor_tensor(out=gap[:], in0=by_slot(p_acc), in1=q_sb[c][:], op=ALU.subtract)
+            th.append(sb.tile([P, PACK, P], F32, name="th%d" % c))
+            nc.scalar.activation(out=th[c][:], in_=gap[:], func=ACT.Tanh)
+
+        turned = []
+        for c in range(TILES):
+            turned.append(bank(c))
+            for j in range(PACK):
+                nc.tensor.transpose(turned[c][:, j * P : (j + 1) * P], th[c][:, j, :], ident[:])
+
+        for h in range(2):
+            d_bf = {}
+            for c in (2 * h, 2 * h + 1):
+                d_bf[c] = sb.tile([P, P, PACK], BF16, name="d_bf%d" % c, align_bytes=64)
+                nc.vector.tensor_tensor(
+                    out=d_bf[c][:],
+                    in0=turned[c][:].rearrange("p (j t) -> p t j", j=PACK),
+                    in1=us_sb[:].unsqueeze(1).to_broadcast([P, P, PACK]),
+                    op=ALU.mult,
+                )
+            for c in (2 * h, 2 * h + 1):
+                cols = slice(HALF + c * P, HALF + (c + 1) * P)
+                nc.vector.quantize_mx(
+                    out=d_codes[:, cols].bitcast(E5M2),
+                    scales=d_scales[:, cols],
+                    in_=d_bf[c][:].rearrange("p t j -> p (t j)"),
+                )
+
+        for h in range(2):
+            window = slice(h * HALF, h * HALF + D)
+            tokens = slice(h * HALF, (h + 1) * HALF)
+            for i in range(TILES):
+                b_acc = bank((1 - h) * TILES + i)
+                nc.tensor.matmul_mx(
+                    out=b_acc[:],
+                    lhsT=wt[:, i * PACK * P : (i + 1) * PACK * P].bitcast(E4M3),
+                    lhsT_scale=wt_s[:, i * P : (i + 1) * P],
+                    rhs=d_codes[:, window].bitcast(E5M2),
+                    rhs_scale=d_scales[:, window],
+                    start=True,
+                    stop=True,
+                )
+                res = sb.tile([P, HALF], F32, name="res%d_%d" % (h, i))
+                nc.vector.tensor_tensor(out=res[:], in0=b_acc[:, HALF:], in1=rw_sb[:, tokens], op=ALU.mult)
+                nc.sync.dma_start(out=out[i * P : (i + 1) * P, tokens], in_=res[:])

@@ -37,56 +37,56 @@ def tile_mix_gap_of_two_sums_back_kernel(
             nc.vector.memset(planes[:].bitcast(I32), 0)
             return planes
 
-        def stage_scales(name, scale_inputs):
+        def stage_scales(queue, name, scale_inputs):
             staged = sb.tile([P, len(scale_inputs), D // 4], I32, name=name)
             for i, scales in enumerate(scale_inputs):
-                nc.sync.dma_start(out=staged[16:32, i, :], in_=scales[0].bitcast(I32))
+                queue.dma_start(out=staged[16:32, i, :], in_=scales[0].bitcast(I32))
             return staged
 
-        def spread_scales(planes, staged):
+        def spread_scales(queue, planes, staged):
             for q in range(4):
-                nc.sync.dma_start(
+                queue.dma_start(
                     out=planes[32 * q : 32 * q + 4].bitcast(I32), in_=staged[16 + 4 * q : 20 + 4 * q]
                 )
 
-        def load_codes(name, rows):
+        def load_codes(queue, name, rows):
             codes = sb.tile([P, rows.shape[1]], U8, name=name, align_bytes=64)
-            nc.sync.dma_start(out=codes[:].bitcast(I32), in_=rows.bitcast(I32))
+            queue.dma_start(out=codes[:].bitcast(I32), in_=rows.bitcast(I32))
             return codes
 
         def fp8_rows(words):
             return words[0].rearrange("p n r -> p (n r)")
 
-        q_planes = zeroed_planes("q_planes", 4)
-        p_planes = zeroed_planes("p_planes", 2)
-        wt_plane = zeroed_planes("wt_plane", 1)
-        d_codes = sb.tile([P, HALF + D], U32, align_bytes=64)
-        d_scales = sb.tile([P, HALF + D], U8, align_bytes=64)
-        nc.vector.memset(d_codes[:, :HALF], 0)
-        nc.vector.memset(d_scales[:, :HALF].bitcast(U32), 0)
         first = sb.tile([P, 2], F32)
-        nc.vector.memset(first[:, 0:1], 0.0)
+        nc.gpsimd.memset(first[:, 0:1], 0.0)
         nc.scalar.activation(out=first[:, 1:2], in_=first[:, 0:1], func=ACT.Tanh)
         ident = sb.tile([P, P], F32)
         make_identity(nc, ident[:])
+        d_codes = sb.tile([P, HALF + D], U32, align_bytes=64)
+        d_scales = sb.tile([P, HALF + D], U8, align_bytes=64)
+        nc.vector.memset(d_scales[:, :D].bitcast(U32), 0)
+        nc.vector.memset(d_codes[:, :D], 0)
+        q_planes = zeroed_planes("q_planes", 4)
+        p_planes = zeroed_planes("p_planes", 2)
+        wt_plane = zeroed_planes("wt_plane", 1)
 
-        q_staged = stage_scales("q_staged", (xt_scales, wb_scales, xq_scales, we_scales))
-        xt = load_codes("xt", fp8_rows(xt_words))
-        wb = load_codes("wb", wb_words[0])
-        xq = load_codes("xq", fp8_rows(xq_words))
-        we = load_codes("we", fp8_rows(we_words))
-        spread_scales(q_planes, q_staged)
-        p_staged = stage_scales("p_staged", (wa_scales, wc_scales))
-        wa = load_codes("wa", wa_words[0])
-        wc = load_codes("wc", wc_words[0])
-        spread_scales(p_planes, p_staged)
-        wt_staged = stage_scales("wt_staged", (wt_scales,))
+        q_staged = stage_scales(nc.sync, "q_staged", (xt_scales, wb_scales, xq_scales, we_scales))
+        xt = load_codes(nc.sync, "xt", fp8_rows(xt_words))
+        wb = load_codes(nc.sync, "wb", wb_words[0])
+        xq = load_codes(nc.sync, "xq", fp8_rows(xq_words))
+        we = load_codes(nc.sync, "we", fp8_rows(we_words))
+        spread_scales(nc.scalar, q_planes, q_staged)
+        p_staged = stage_scales(nc.scalar, "p_staged", (wa_scales, wc_scales))
+        wa = load_codes(nc.scalar, "wa", wa_words[0])
+        wc = load_codes(nc.scalar, "wc", wc_words[0])
+        spread_scales(nc.sync, p_planes, p_staged)
+        wt_staged = stage_scales(nc.sync, "wt_staged", (wt_scales,))
         us_sb = sb.tile([P, PACK], F32)
         nc.sync.dma_start(out=us_sb[:], in_=us.rearrange("(p j) o -> p (j o)", j=PACK))
-        wt = load_codes("wt", fp8_rows(wt_words))
-        spread_scales(wt_plane, wt_staged)
-        rw_sb = sb.tile([P, D], F32)
-        nc.sync.dma_start(out=rw_sb[:], in_=rw[0].partition_broadcast(P))
+        rw_col = sb.tile([P, PACK], F32)
+        nc.sync.dma_start(out=rw_col[:], in_=rw.rearrange("o (p j) -> p (o j)", j=PACK))
+        wt = load_codes(nc.sync, "wt", fp8_rows(wt_words))
+        spread_scales(nc.sync, wt_plane, wt_staged)
         xt_s, wb_s, xq_s, we_s = [q_planes[:, i, :] for i in range(4)]
         wa_s, wc_s = [p_planes[:, i, :] for i in range(2)]
         wt_s = wt_plane[:, 0, :]
@@ -94,6 +94,13 @@ def tile_mix_gap_of_two_sums_back_kernel(
         def bank(i):
             acc = ps.tile([P, D], F32, name="acc", tag="bank%d" % i)
             return acc
+
+        idle = bank(7)
+        for w in range(7):
+            nc.tensor.matmul_mx(
+                out=idle[:], lhsT=d_codes[:, :P].bitcast(E4M3), lhsT_scale=d_scales[:, :P],
+                rhs=d_codes[:, :D].bitcast(E5M2), rhs_scale=d_scales[:, :D], start=True, stop=True,
+            )
 
         def product(acc, c, x, x_s, w, w_s, w_dtype, opens):
             nc.tensor.matmul_mx(
@@ -133,6 +140,22 @@ def tile_mix_gap_of_two_sums_back_kernel(
             turned.append(bank(c))
             for j in range(PACK):
                 nc.tensor.transpose(turned[c][:, j * P : (j + 1) * P], th[c][:, j, :], ident[:])
+            if c == 1:
+                rw_acc = bank(TILES)
+                for j in range(PACK):
+                    nc.tensor.transpose(
+                        rw_acc[:, j * P : (j + 1) * P], rw_col[:, j : j + 1].to_broadcast([P, P]), ident[:]
+                    )
+                idle = bank(TILES + 1)
+                for w in range(2):
+                    nc.tensor.matmul_mx(
+                        out=idle[:], lhsT=xt[:, : PACK * P].bitcast(E4M3), lhsT_scale=xt_s[:, :P],
+                        rhs=wb[:].bitcast(E2M1), rhs_scale=wb_s, start=True, stop=True,
+                    )
+        rw_sb = sb.tile([P, D], F32)
+        nc.scalar.copy(
+            out=rw_sb[:].rearrange("p (n j) -> p n j", j=PACK), in_=rw_acc[:].rearrange("p (j n) -> p n j", j=PACK)
+        )
 
         for h in range(2):
             d_bf = {}

@@ -44,7 +44,7 @@ def tile_mix_gap_of_two_sums_back_kernel(
             return staged
 
         def spread_scales(queue, planes, staged):
-            for q in range(4):
+            for q in (0, 2, 1, 3):
                 queue.dma_start(
                     out=planes[32 * q : 32 * q + 4].bitcast(I32), in_=staged[16 + 4 * q : 20 + 4 * q]
                 )
@@ -66,20 +66,19 @@ def tile_mix_gap_of_two_sums_back_kernel(
         d_scales = sb.tile([P, HALF + D], U8, align_bytes=64)
         nc.vector.memset(d_scales[:, :D].bitcast(U32), 0)
         nc.vector.memset(d_codes[:, :D], 0)
-        q_planes = zeroed_planes("q_planes", 4)
-        p_planes = zeroed_planes("p_planes", 2)
+        planes = zeroed_planes("planes", 6)
         wt_plane = zeroed_planes("wt_plane", 1)
 
-        q_staged = stage_scales(nc.sync, "q_staged", (xt_scales, wb_scales, xq_scales, we_scales))
+        staged = stage_scales(
+            nc.sync, "staged", (xt_scales, wb_scales, xq_scales, we_scales, wa_scales, wc_scales)
+        )
         xt = load_codes(nc.sync, "xt", fp8_rows(xt_words))
         wb = load_codes(nc.sync, "wb", wb_words[0])
+        spread_scales(nc.sync, planes, staged)
         xq = load_codes(nc.sync, "xq", fp8_rows(xq_words))
         we = load_codes(nc.sync, "we", fp8_rows(we_words))
-        spread_scales(nc.scalar, q_planes, q_staged)
-        p_staged = stage_scales(nc.scalar, "p_staged", (wa_scales, wc_scales))
-        wa = load_codes(nc.scalar, "wa", wa_words[0])
-        wc = load_codes(nc.scalar, "wc", wc_words[0])
-        spread_scales(nc.sync, p_planes, p_staged)
+        wa = load_codes(nc.sync, "wa", wa_words[0])
+        wc = load_codes(nc.sync, "wc", wc_words[0])
         wt_staged = stage_scales(nc.sync, "wt_staged", (wt_scales,))
         us_sb = sb.tile([P, PACK], F32)
         nc.sync.dma_start(out=us_sb[:], in_=us.rearrange("(p j) o -> p (j o)", j=PACK))
@@ -87,8 +86,7 @@ def tile_mix_gap_of_two_sums_back_kernel(
         nc.sync.dma_start(out=rw_col[:], in_=rw.rearrange("o (p j) -> p (o j)", j=PACK))
         wt = load_codes(nc.sync, "wt", fp8_rows(wt_words))
         spread_scales(nc.sync, wt_plane, wt_staged)
-        xt_s, wb_s, xq_s, we_s = [q_planes[:, i, :] for i in range(4)]
-        wa_s, wc_s = [p_planes[:, i, :] for i in range(2)]
+        xt_s, wb_s, xq_s, we_s, wa_s, wc_s = [planes[:, i, :] for i in range(6)]
         wt_s = wt_plane[:, 0, :]
 
         def bank(i):
@@ -96,7 +94,7 @@ def tile_mix_gap_of_two_sums_back_kernel(
             return acc
 
         idle = bank(7)
-        for w in range(7):
+        for w in range(6):
             nc.tensor.matmul_mx(
                 out=idle[:], lhsT=d_codes[:, :P].bitcast(E4M3), lhsT_scale=d_scales[:, :P],
                 rhs=d_codes[:, :D].bitcast(E5M2), rhs_scale=d_scales[:, :D], start=True, stop=True,
@@ -157,38 +155,57 @@ def tile_mix_gap_of_two_sums_back_kernel(
             out=rw_sb[:].rearrange("p (n j) -> p n j", j=PACK), in_=rw_acc[:].rearrange("p (j n) -> p n j", j=PACK)
         )
 
-        for h in range(2):
-            d_bf = {}
-            for c in (2 * h, 2 * h + 1):
-                d_bf[c] = sb.tile([P, P, PACK], BF16, name="d_bf%d" % c, align_bytes=64)
-                nc.vector.tensor_tensor(
-                    out=d_bf[c][:],
-                    in0=turned[c][:].rearrange("p (j t) -> p t j", j=PACK),
-                    in1=us_sb[:].unsqueeze(1).to_broadcast([P, P, PACK]),
-                    op=ALU.mult,
-                )
-            for c in (2 * h, 2 * h + 1):
-                cols = slice(HALF + c * P, HALF + (c + 1) * P)
-                nc.vector.quantize_mx(
-                    out=d_codes[:, cols].bitcast(E5M2),
-                    scales=d_scales[:, cols],
-                    in_=d_bf[c][:].rearrange("p t j -> p (t j)"),
-                )
+        d_bf = {}
 
-        for h in range(2):
-            window = slice(h * HALF, h * HALF + D)
-            tokens = slice(h * HALF, (h + 1) * HALF)
-            for i in range(TILES):
-                b_acc = bank((1 - h) * TILES + i)
-                nc.tensor.matmul_mx(
-                    out=b_acc[:],
-                    lhsT=wt[:, i * PACK * P : (i + 1) * PACK * P].bitcast(E4M3),
-                    lhsT_scale=wt_s[:, i * P : (i + 1) * P],
-                    rhs=d_codes[:, window].bitcast(E5M2),
-                    rhs_scale=d_scales[:, window],
-                    start=True,
-                    stop=True,
-                )
-                res = sb.tile([P, HALF], F32, name="res%d_%d" % (h, i))
-                nc.vector.tensor_tensor(out=res[:], in0=b_acc[:, HALF:], in1=rw_sb[:, tokens], op=ALU.mult)
-                nc.sync.dma_start(out=out[i * P : (i + 1) * P, tokens], in_=res[:])
+        def weigh(c):
+            d_bf[c] = sb.tile([P, P, PACK], BF16, name="d_bf%d" % c, align_bytes=64)
+            nc.vector.tensor_tensor(
+                out=d_bf[c][:],
+                in0=turned[c][:].rearrange("p (j t) -> p t j", j=PACK),
+                in1=us_sb[:].unsqueeze(1).to_broadcast([P, P, PACK]),
+                op=ALU.mult,
+            )
+
+        def quantise(c):
+            cols = slice(HALF + c * P, HALF + (c + 1) * P)
+            nc.vector.quantize_mx(
+                out=d_codes[:, cols].bitcast(E5M2),
+                scales=d_scales[:, cols],
+                in_=d_bf[c][:].rearrange("p t j -> p (t j)"),
+            )
+
+        def back(i, window_start, bank_index):
+            window = slice(window_start, window_start + D)
+            b_acc = bank(bank_index)
+            nc.tensor.matmul_mx(
+                out=b_acc[:],
+                lhsT=wt[:, i * PACK * P : (i + 1) * PACK * P].bitcast(E4M3),
+                lhsT_scale=wt_s[:, i * P : (i + 1) * P],
+                rhs=d_codes[:, window].bitcast(E5M2),
+                rhs_scale=d_scales[:, window],
+                start=True,
+                stop=True,
+            )
+            return b_acc
+
+        def finish(i, b_cols, t0, width):
+            res = sb.tile([P, width], F32, name="res%d_%d" % (i, t0))
+            nc.vector.tensor_tensor(out=res[:], in0=b_cols, in1=rw_sb[:, t0 : t0 + width], op=ALU.mult)
+            nc.sync.dma_start(out=out[i * P : (i + 1) * P, t0 : t0 + width], in_=res[:])
+
+        last = TILES - 1
+        weigh(0)
+        weigh(1)
+        quantise(0)
+        quantise(1)
+        early = [back(i, 0, TILES + i) for i in range(last)]
+        weigh(2)
+        weigh(3)
+        finish(0, early[0][:, HALF:], 0, HALF)
+        quantise(2)
+        quantise(3)
+        for i in range(1, last):
+            finish(i, early[i][:, HALF:], 0, HALF)
+        finish(last, back(last, HALF, TILES + last)[:], 0, D)
+        for i in range(last):
+            finish(i, back(i, HALF, i)[:, HALF:], HALF, HALF)

from contextlib import ExitStack

import concourse.mybir as mybir
from concourse.masks import make_identity

F32 = mybir.dt.float32
BF16 = mybir.dt.bfloat16
I32 = mybir.dt.int32
U32 = mybir.dt.uint32
U8 = mybir.dt.uint8
E4M3 = mybir.dt.float8_e4m3fn_x4
E5M2 = mybir.dt.float8_e5m2_x4
E2M1 = mybir.dt.float4_e2m1fn_x4
ACT = mybir.ActivationFunctionType
ALU = mybir.AluOpType

P = 128
D = 512
PACK = 4
TILES = D // P
HALF = D // 2
FLOPS = 5 * 2 * D * D * D


def tile_mix_gap_of_two_sums_back_kernel(
    tc, xt_words, xt_scales, wa_words, wa_scales, xq_words, xq_scales, wc_words, wc_scales,
    wb_words, wb_scales, we_words, we_scales, us, wt_words, wt_scales, rw, out,
):
    nc = tc.nc
    with ExitStack() as ctx:
        sb = ctx.enter_context(tc.tile_pool(name="sb", bufs=1))
        ps = ctx.enter_context(tc.psum_pool(name="ps", bufs=1))
        ctx.enter_context(tc.manual_schedule())

        def zeroed_planes(name, count):
            planes = sb.tile([P, count, D], U8, name=name, align_bytes=64)
            nc.vector.memset(planes[:].bitcast(I32), 0)
            return planes

        def stage_scales(queue, name, scale_inputs):
            staged = sb.tile([P, len(scale_inputs), D // 4], I32, name=name)
            for i, scales in enumerate(scale_inputs):
                queue.dma_start(out=staged[16:32, i, :], in_=scales[0].bitcast(I32))
            return staged

        def spread_scales(queue, planes, staged):
            for q in (0, 2, 1, 3):
                queue.dma_start(
                    out=planes[32 * q : 32 * q + 4].bitcast(I32), in_=staged[16 + 4 * q : 20 + 4 * q]
                )

        def load_codes(queue, name, rows):
            codes = sb.tile([P, rows.shape[1]], U8, name=name, align_bytes=64)
            queue.dma_start(out=codes[:].bitcast(I32), in_=rows.bitcast(I32))
            return codes

        def fp8_rows(words):
            return words[0].rearrange("p n r -> p (n r)")

        first = sb.tile([P, 2], F32)
        nc.gpsimd.memset(first[:, 0:1], 0.0)
        nc.scalar.activation(out=first[:, 1:2], in_=first[:, 0:1], func=ACT.Tanh)
        ident = sb.tile([P, P], F32)
        make_identity(nc, ident[:])
        d_codes = sb.tile([P, HALF + D], U32, align_bytes=64)
        d_scales = sb.tile([P, HALF + D], U8, align_bytes=64)
        nc.vector.memset(d_scales[:, :D].bitcast(U32), 0)
        nc.vector.memset(d_codes[:, :D], 0)
        planes = zeroed_planes("planes", 6)
        wt_plane = zeroed_planes("wt_plane", 1)

        staged = stage_scales(
            nc.sync, "staged", (xt_scales, wb_scales, xq_scales, we_scales, wa_scales, wc_scales)
        )
        xt = load_codes(nc.sync, "xt", fp8_rows(xt_words))
        wb = load_codes(nc.sync, "wb", wb_words[0])
        spread_scales(nc.sync, planes, staged)
        xq = load_codes(nc.sync, "xq", fp8_rows(xq_words))
        we = load_codes(nc.sync, "we", fp8_rows(we_words))
        wa = load_codes(nc.sync, "wa", wa_words[0])
        wc = load_codes(nc.sync, "wc", wc_words[0])
        wt_staged = stage_scales(nc.sync, "wt_staged", (wt_scales,))
        us_sb = sb.tile([P, PACK], F32)
        nc.sync.dma_start(out=us_sb[:], in_=us.rearrange("(p j) o -> p (j o)", j=PACK))
        rw_col = sb.tile([P, PACK], F32)
        nc.sync.dma_start(out=rw_col[:], in_=rw.rearrange("o (p j) -> p (o j)", j=PACK))
        wt = load_codes(nc.sync, "wt", fp8_rows(wt_words))
        spread_scales(nc.sync, wt_plane, wt_staged)
        xt_s, wb_s, xq_s, we_s, wa_s, wc_s = [planes[:, i, :] for i in range(6)]
        wt_s = wt_plane[:, 0, :]

        def bank(i):
            acc = ps.tile([P, D], F32, name="acc", tag="bank%d" % i)
            return acc

        idle = bank(7)
        for w in range(6):
            nc.tensor.matmul_mx(
                out=idle[:], lhsT=d_codes[:, :P].bitcast(E4M3), lhsT_scale=d_scales[:, :P],
                rhs=d_codes[:, :D].bitcast(E5M2), rhs_scale=d_scales[:, :D], start=True, stop=True,
            )

        def product(acc, c, x, x_s, w, w_s, w_dtype, opens):
            nc.tensor.matmul_mx(
                out=acc[:],
                lhsT=x[:, c * PACK * P : (c + 1) * PACK * P].bitcast(E4M3),
                lhsT_scale=x_s[:, c * P : (c + 1) * P],
                rhs=w[:].bitcast(w_dtype),
                rhs_scale=w_s,
                start=opens,
                stop=not opens,
            )

        def by_slot(acc):
            return acc[:].rearrange("t (p j) -> t j p", j=PACK)

        q_acc = [bank(c) for c in range(TILES)]
        for c in range(TILES):
            product(q_acc[c], c, xt, xt_s, wb, wb_s, E2M1, True)
        q_sb = []
        for c in range(TILES):
            product(q_acc[c], c, xq, xq_s, we, we_s, E4M3, False)
            q_sb.append(sb.tile([P, PACK, P], F32, name="q_sb%d" % c))
            nc.scalar.copy(out=q_sb[c][:], in_=by_slot(q_acc[c]))

        th = []
        for c in range(TILES):
            p_acc = bank(TILES + c)
            product(p_acc, c, xt, xt_s, wa, wa_s, E2M1, True)
            product(p_acc, c, xq, xq_s, wc, wc_s, E2M1, False)
            gap = sb.tile([P, PACK, P], F32, name="gap%d" % c)
            nc.vector.tensor_tensor(out=gap[:], in0=by_slot(p_acc), in1=q_sb[c][:], op=ALU.subtract)
            th.append(sb.tile([P, PACK, P], F32, name="th%d" % c))
            nc.scalar.activation(out=th[c][:], in_=gap[:], func=ACT.Tanh)

        turned = []
        for c in range(TILES):
            turned.append(bank(c))
            for j in range(PACK):
                nc.tensor.transpose(turned[c][:, j * P : (j + 1) * P], th[c][:, j, :], ident[:])
            if c == 1:
                rw_acc = bank(TILES)
                for j in range(PACK):
                    nc.tensor.transpose(
                        rw_acc[:, j * P : (j + 1) * P], rw_col[:, j : j + 1].to_broadcast([P, P]), ident[:]
                    )
                idle = bank(TILES + 1)
                for w in range(2):
                    nc.tensor.matmul_mx(
                        out=idle[:], lhsT=xt[:, : PACK * P].bitcast(E4M3), lhsT_scale=xt_s[:, :P],
                        rhs=wb[:].bitcast(E2M1), rhs_scale=wb_s, start=True, stop=True,
                    )
        rw_sb = sb.tile([P, D], F32)
        nc.scalar.copy(
            out=rw_sb[:].rearrange("p (n j) -> p n j", j=PACK), in_=rw_acc[:].rearrange("p (j n) -> p n j", j=PACK)
        )

        d_bf = {}

        def weigh(c):
            d_bf[c] = sb.tile([P, P, PACK], BF16, name="d_bf%d" % c, align_bytes=64)
            nc.vector.tensor_tensor(
                out=d_bf[c][:],
                in0=turned[c][:].rearrange("p (j t) -> p t j", j=PACK),
                in1=us_sb[:].unsqueeze(1).to_broadcast([P, P, PACK]),
                op=ALU.mult,
            )

        def quantise(c):
            cols = slice(HALF + c * P, HALF + (c + 1) * P)
            nc.vector.quantize_mx(
                out=d_codes[:, cols].bitcast(E5M2),
                scales=d_scales[:, cols],
                in_=d_bf[c][:].rearrange("p t j -> p (t j)"),
            )

        def back(i, window_start, bank_index):
            window = slice(window_start, window_start + D)
            b_acc = bank(bank_index)
            nc.tensor.matmul_mx(
                out=b_acc[:],
                lhsT=wt[:, i * PACK * P : (i + 1) * PACK * P].bitcast(E4M3),
                lhsT_scale=wt_s[:, i * P : (i + 1) * P],
                rhs=d_codes[:, window].bitcast(E5M2),
                rhs_scale=d_scales[:, window],
                start=True,
                stop=True,
            )
            return b_acc

        def finish(i, b_cols, t0, width):
            res = sb.tile([P, width], F32, name="res%d_%d" % (i, t0))
            nc.vector.tensor_tensor(out=res[:], in0=b_cols, in1=rw_sb[:, t0 : t0 + width], op=ALU.mult)
            nc.sync.dma_start(out=out[i * P : (i + 1) * P, t0 : t0 + width], in_=res[:])

        last = TILES - 1
        weigh(0)
        weigh(1)
        quantise(0)
        quantise(1)
        early = [back(i, 0, TILES + i) for i in range(last)]
        weigh(2)
        weigh(3)
        finish(0, early[0][:, HALF:], 0, HALF)
        quantise(2)
        quantise(3)
        for i in range(1, last):
            finish(i, early[i][:, HALF:], 0, HALF)
        finish(last, back(last, HALF, TILES + last)[:], 0, D)
        for i in range(last):
            finish(i, back(i, HALF, i)[:, HALF:], HALF, HALF)
